import numpy as np
import ml_dtypes


def mxq(x, axis, fmt="e4m3"):
    dtype, down = {"e4m3": (ml_dtypes.float8_e4m3fn, 7), "e5m2": (ml_dtypes.float8_e5m2, 14)}[fmt]
    v = np.moveaxis(np.asarray(x, np.float32).astype(ml_dtypes.bfloat16).astype(np.float64), axis, -1)
    blocks = v.reshape(v.shape[:-1] + (-1, 32))
    amax = np.abs(blocks).max(-1, keepdims=True)
    byte = np.maximum(np.where(amax > 0, np.frexp(amax)[1] - 1 + 127, 0) - down, 1)
    scale = np.exp2(byte - 127.0)
    codes = (blocks / scale).astype(np.float32).astype(dtype).astype(np.float64)
    return np.moveaxis((codes * scale).reshape(v.shape), -1, axis)


WIDE = False


def mx_kscale(k):
    if not WIDE:
        return np.ones(k)
    levels = np.array([10, -10, 5, -5, 0])
    if k % 512:
        return np.exp2(np.random.permutation(np.resize(levels, k // 32))).repeat(32)
    a = np.empty((k // 512, 16))
    for p in range(k // 512):
        a[p, :8] = np.random.permutation(np.resize(levels, 8))
        for g in range(8):
            far = levels[np.abs(levels - a[p, g]) >= 10]
            a[p, g + 8] = far[np.random.randint(len(far))]
    return np.exp2(a.ravel()).repeat(32)


def f64(x):
    return np.asarray(x).astype(np.float64)


def striped(idx):
    return np.tile(idx.reshape(-1, 16).T, (8, 1)).astype(np.uint16)


def unstriped(offs):
    return offs[:16].T.reshape(-1).astype(np.int64)


def striped8(idx):
    return np.concatenate([x.reshape(-1, 16).T for x in idx]).astype(np.uint16)


def runs(offs, k):
    lists = np.stack([offs[16 * r : 16 * r + 16].T.reshape(-1) for r in range(8)]).astype(np.int64)
    return lists[np.arange(k) % 512 // 64]


def pack_weight(w):
    k, n = w.shape
    w = f64(np.asarray(w, np.float32).astype(ml_dtypes.bfloat16)).reshape(k // 32, 32, n)
    amax = np.abs(w).max(1)
    byte = np.clip(np.where(amax > 0, np.frexp(amax)[1] - 1 + 127 - 7, 1), 1, 254)
    scaled = (w * np.exp2(127.0 - byte)[:, None, :]).reshape(k, n).astype(np.float32)
    words = np.ascontiguousarray(scaled.reshape(k // 512, 128, 4, n).transpose(0, 1, 3, 2)).astype(ml_dtypes.float8_e4m3fn).view(np.uint8)
    return words, np.ascontiguousarray(byte.astype(np.uint8).reshape(k // 512, 16, n))


def unpack_weight(words, scales):
    g, p, n, _ = words.shape
    vals = np.ascontiguousarray(words).view(ml_dtypes.float8_e4m3fn).astype(np.float64) * np.repeat(np.exp2(scales.astype(np.float64) - 127.0), 8, axis=1)[..., None]
    return vals.transpose(0, 1, 3, 2).reshape(g * 512, n)


E2M1 = np.array([0.0, 0.5, 1.0, 1.5, 2.0, 3.0, 4.0, 6.0, -0.0, -0.5, -1.0, -1.5, -2.0, -3.0, -4.0, -6.0])


def pack_fp4(w):
    k, n = w.shape
    w = f64(np.asarray(w, np.float32).astype(ml_dtypes.bfloat16)).reshape(k // 32, 32, n)
    amax = np.abs(w).max(1)
    mant, ex = np.frexp(amax / 6.0)
    byte = np.clip(np.where(amax > 0, np.where(mant > 0.5, ex, ex - 1) + 127, 1), 1, 254)
    scaled = (w * np.exp2(127.0 - byte)[:, None, :]).reshape(k, n).astype(np.float32)
    c = np.ascontiguousarray(scaled.reshape(k // 512, 128, 4, n).transpose(0, 1, 3, 2)).astype(ml_dtypes.float4_e2m1fn).view(np.uint8) & 0xF
    words = (c[..., 0::2] | (c[..., 1::2] << 4)).reshape(k // 512, 128, 2 * n)
    return np.ascontiguousarray(words), np.ascontiguousarray(byte.astype(np.uint8).reshape(k // 512, 16, n))


def unpack_fp4(words, scales):
    g, _, n = scales.shape
    words = np.ascontiguousarray(words).reshape(g, 128, n, 2)
    nib = np.empty((g, 128, n, 4), np.uint8)
    nib[..., 0::2] = words & 0xF
    nib[..., 1::2] = words >> 4
    vals = E2M1[nib] * np.repeat(np.exp2(scales.astype(np.float64) - 127.0), 8, axis=1)[..., None]
    return vals.transpose(0, 1, 3, 2).reshape(g * 512, n)


def planes(y):
    n, m = y.shape
    v = y.astype(np.float32).astype(ml_dtypes.bfloat16).astype(np.float64).reshape(n // 32, 32, m)
    top = np.abs(v).max(1)
    byte = np.clip(np.where(top > 0, np.frexp(top)[1] - 1 + 127 - 7, 1), 1, 254)
    codes = (v * np.exp2(127.0 - byte)[:, None, :]).reshape(n, m).astype(np.float32).astype(ml_dtypes.float8_e4m3fn).view(np.uint8)
    words = codes.reshape(n // 512, 128, 4, m).transpose(0, 1, 3, 2)
    return np.ascontiguousarray(words), np.ascontiguousarray(byte.astype(np.uint8).reshape(n // 512, 16, m))


K, T, S, N, H, C = 512, 2048, 512, 512, 512, 512


def setup_inputs():
    n = np.random.standard_normal
    s = mx_kscale(K)[:, None]
    u = mx_kscale(S)
    packed_xT = pack_weight(n((K, T)) * s)
    packed_w1 = pack_fp4(n((K, H)) / np.sqrt(K) / s)
    packed_w2 = pack_fp4(n((K, H)) / np.sqrt(K) / s)
    packed_w3 = pack_fp4(n((H, N)) / np.sqrt(H) / u[:, None])
    return {
        "x_words": packed_xT[0],
        "x_scales": packed_xT[1],
        "w1_words": packed_w1[0],
        "w1_scales": packed_w1[1],
        "w2_words": packed_w2[0],
        "w2_scales": packed_w2[1],
        "gn": (np.random.uniform(0.5, 1.5, (H, 1)) * u[:, None]).astype(np.float32),
        "w3_words": packed_w3[0],
        "w3_scales": packed_w3[1],
        "gs": (np.random.uniform(0.5, 1.5, (K, 1)) / s).astype(np.float32),
        "offs": striped(np.random.permutation(T)[:S]),
        "two": striped(np.random.permutation(T)[:S]),
        "n1": striped8(np.stack([np.random.permutation(S) for _ in range(8)])),
        "n2": striped8(np.stack([np.random.permutation(S) for _ in range(8)])),
        "n3": striped8(np.stack([np.random.permutation(S) for _ in range(8)])),
        "cand": striped(np.random.permutation(T)[:C]),
        "n4": striped8(np.stack([np.random.permutation(S) for _ in range(8)])),
        "n5": striped8(np.stack([np.random.permutation(S) for _ in range(8)])),
        "n6": striped8(np.stack([np.random.permutation(S) for _ in range(8)])),
    }


def reference(x_words, x_scales, w1_words, w1_scales, w2_words, w2_scales, gn, w3_words, w3_scales, gs, offs, two, n1, n2, n3, cand, n4, n5, n6):
    x_cand = unpack_weight(x_words, x_scales)[:, unstriped(cand)]
    x_two = unpack_weight(x_words, x_scales)[:, unstriped(two)]
    d = unpack_fp4(w2_words, w2_scales).T @ x_two
    z2 = f64(gs) * (d / (np.abs(d[np.arange(H)[:, None], runs(n3, H)]) + 0.5))
    b = 0.0625 * ((x_cand.T @ mxq(z2, 0, "e4m3")))
    xq = unpack_weight(x_words, x_scales)[:, unstriped(offs)]
    y = unpack_fp4(w1_words, w1_scales).T @ xq
    z = f64(gn) * ((np.tanh(y[np.arange(H)[:, None], runs(n1, H)] - y)) * (y[np.arange(H)[:, None], runs(n2, H)]))
    a = unpack_fp4(w3_words, w3_scales).T @ mxq(z, 0, "e4m3")
    out_0 = b * (a[np.arange(N)[:, None], runs(n4, N)] - a) + 0.5 * ((b[np.arange(C)[:, None], runs(n6, C)]) * (a[np.arange(N)[:, None], runs(n5, N)] - a))
    return (out_0,) + planes(out_0)

@@ -1,0 +1,291 @@
+from contextlib import ExitStack
+
+import concourse.mybir as mybir
+
+F32 = mybir.dt.float32
+BF16 = mybir.dt.bfloat16
+I32 = mybir.dt.int32
+U32 = mybir.dt.uint32
+U16 = mybir.dt.uint16
+U8 = mybir.dt.uint8
+FP8X4 = mybir.dt.float8_e4m3fn_x4
+FP4X4 = mybir.dt.float4_e2m1fn_x4
+ALU = mybir.AluOpType
+ACT = mybir.ActivationFunctionType
+
+P = 128
+PACK = 4
+T = 2048
+S = 512
+HALF = 256
+HALVES = S // HALF
+LCOLS = HALF // 16
+FLOPS = 4 * 2 * 512 * 512 * 512
+
+
+def tile_picked_tfcdflowbfdifnorm_none_po_kernel(
+    tc, x_words, x_scales, w1_words, w1_scales, w2_words, w2_scales, gn, w3_words, w3_scales, gs,
+    offs, two, n1, n2, n3, cand, n4, n5, n6, out_0, out_1, out_2,
+):
+    nc = tc.nc
+    with ExitStack() as ctx:
+        keep = ctx.enter_context(tc.tile_pool(name="keep", bufs=1))
+        psum = ctx.enter_context(tc.psum_pool(name="psum", bufs=1))
+
+        def sb(name, shape, dtype):
+            return keep.tile(shape, dtype, name=name, align_bytes=64)
+
+        def load_list(name, src):
+            tile = keep.tile([P, S // 16], U16, name=name)
+            nc.sync.dma_start(tile[:], src)
+            return tile
+
+        def load_scale_rows(queue, tile, src):
+            for q in range(4):
+                queue.dma_start(tile[32 * q : 32 * q + 4, :].bitcast(I32), src[0, 4 * q : 4 * q + 4, :].bitcast(I32))
+
+        def load_w_words(name, src):
+            tile = sb(name, [P, 2 * S], U8)
+            nc.sync.dma_start(tile[:].bitcast(I32), src[0].bitcast(I32))
+            return tile
+
+        def half(lst, h):
+            return lst[:, h * LCOLS : (h + 1) * LCOLS]
+
+        def cols(h):
+            return slice(h * HALF, (h + 1) * HALF)
+
+        xs = sb("xs", [P, T], U8)
+        nc.gpsimd.memset(xs[:].bitcast(I32), 0)
+        wsraw = [sb(f"wsraw{i}", [P, S], U8) for i in range(3)]
+        for i in range(3):
+            nc.gpsimd.memset(wsraw[i][:].bitcast(I32), 0)
+        load_scale_rows(nc.scalar, xs, x_scales)
+        l_offs = load_list("l_offs", offs)
+        xw = sb("xw", [P, T], I32)
+        nc.sync.dma_start(xw[:], x_words[0].rearrange("p n t -> p (n t)").bitcast(I32))
+        w1raw = load_w_words("w1raw", w1_words)
+        load_scale_rows(nc.sync, wsraw[0], w1_scales)
+        l_two = load_list("l_two", two)
+        gn_t = sb("gn_t", [P, PACK], F32)
+        nc.sync.dma_start(gn_t[:], gn.rearrange("(p t) o -> p (t o)", t=PACK))
+        w2raw = load_w_words("w2raw", w2_words)
+        load_scale_rows(nc.gpsimd, wsraw[1], w2_scales)
+        l_n1 = load_list("l_n1", n1)
+        w3raw = load_w_words("w3raw", w3_words)
+        load_scale_rows(nc.sync, wsraw[2], w3_scales)
+        l_n2 = load_list("l_n2", n2)
+        l_n3 = load_list("l_n3", n3)
+        gs_t = sb("gs_t", [P, PACK], F32)
+        nc.sync.dma_start(gs_t[:], gs.rearrange("(p t) o -> p (t o)", t=PACK))
+        l_cand = load_list("l_cand", cand)
+        l_n4 = load_list("l_n4", n4)
+        l_n5 = load_list("l_n5", n5)
+        l_n6 = load_list("l_n6", n6)
+
+        def gather_scales(name, lst):
+            tile = sb(name, [P, S], U8)
+            nc.vector.tensor_copy(tile[:], xs[:].indirect(lst[:]))
+            return tile
+
+        def gather_words(name, lst):
+            tile = sb(name, [P, S], U32)
+            nc.vector.tensor_copy(tile[:], xw[:].bitcast(U32).indirect(lst[:]))
+            return tile
+
+        def deal_words(name, raw):
+            tile = sb(name, [P, 2 * S], U8)
+            nc.scalar.copy(
+                tile[:].bitcast(U16).rearrange("p (t m) -> p t m", t=PACK),
+                raw[:].bitcast(U16).rearrange("p (m t) -> p t m", t=PACK),
+            )
+            return tile
+
+        def deal(engine, name, raw, dtype):
+            tile = sb(name, [P, S], dtype)
+            engine.tensor_copy(
+                tile[:].rearrange("p (t m) -> p t m", t=PACK),
+                raw[:].rearrange("p (m t) -> p t m", t=PACK),
+            )
+            return tile
+
+        xs_offs = gather_scales("xs_offs", l_offs)
+        xw_offs = gather_words("xw_offs", l_offs)
+        xs_two = gather_scales("xs_two", l_two)
+        xw_two = gather_words("xw_two", l_two)
+        w1 = deal_words("w1", w1raw)
+        w1s = deal(nc.vector, "w1s", wsraw[0], U8)
+        w2 = deal_words("w2", w2raw)
+        w2s = deal(nc.gpsimd, "w2s", wsraw[1], U8)
+        w3 = deal_words("w3", w3raw)
+        w3s = deal(nc.gpsimd, "w3s", wsraw[2], U8)
+
+        gn_safe = sb("gn_safe", [P, PACK], F32)
+        nc.vector.scalar_tensor_tensor(gn_safe[:], gn_t[:], 0.0, gn_t[:], ALU.is_equal, ALU.add)
+        gn_inv = sb("gn_inv", [P, PACK], F32)
+        nc.vector.reciprocal(gn_inv[:], gn_safe[:])
+
+        def mm_w(out, w, ws, t, xq, xq_s):
+            nc.tensor.matmul_mx(
+                out=out,
+                lhsT=w[:, 2 * P * t : 2 * P * (t + 1)].bitcast(FP4X4),
+                lhsT_scale=ws[:, P * t : P * (t + 1)],
+                rhs=xq.bitcast(FP8X4),
+                rhs_scale=xq_s,
+                start=True,
+                stop=True,
+            )
+
+        ywin = [sb(f"ywin{t}", [P, S], F32) for t in range(PACK)]
+        ycopy = [sb(f"ycopy{t}", [P, S], F32) for t in range(PACK)]
+        for t in range(PACK):
+            bank = psum.tile([P, S], F32, name=f"y_bank{t}", tag=f"ya{t}")
+            mm_w(bank[:], w1, w1s, t, xw_offs[:], xs_offs[:])
+            if t < 2:
+                nc.scalar.activation(ywin[t][:], bank[:], ACT.Copy, scale=gn_t[:, t : t + 1])
+            else:
+                nc.vector.tensor_scalar(ywin[t][:], bank[:], gn_t[:, t : t + 1], None, ALU.mult)
+            nc.sync.dma_start(ycopy[t][:], ywin[t][:])
+        d_bank = []
+        absd = sb("absd", [P, PACK, S], F32)
+        for t in range(PACK):
+            bank = psum.tile([P, S], F32, name=f"d_bank{t}", tag=f"db{t}")
+            mm_w(bank[:], w2, w2s, t, xw_two[:], xs_two[:])
+            nc.scalar.activation(absd[:, t, :], bank[:], ACT.Abs)
+            d_bank.append(bank)
+        lwin = [sb(f"lwin{t}", [P, S], F32) for t in range(PACK)]
+        for t in range(PACK):
+            nc.scalar.activation(lwin[t][:], absd[:, t, :], ACT.Ln, bias=0.5)
+
+        xs_cand = gather_scales("xs_cand", l_cand)
+        xw_cand = gather_words("xw_cand", l_cand)
+        cw = deal(nc.vector, "cw", xw_cand, U32)
+        cs = deal(nc.vector, "cs", xs_cand, U8)
+
+        def interleave(engine_copy, dst, src):
+            engine_copy(
+                dst.rearrange("p (c i t) -> p c t i", i=4, t=PACK),
+                src.rearrange("p t (c i) -> p c t i", i=4),
+            )
+
+        diff = sb("diff", [P, HALVES, PACK, HALF], F32)
+        for h in range(HALVES):
+            for t in range(PACK):
+                nc.vector.tensor_tensor(diff[:, h, t, :], ywin[t][:].indirect(half(l_n1, h)), ycopy[t][:, cols(h)], ALU.subtract)
+        for h in range(HALVES):
+            for t in range(PACK):
+                nc.scalar.activation(absd[:, PACK - 1 - t, cols(h)], diff[:, h, t, :], ACT.Tanh, scale=gn_inv[:, t : t + 1])
+        zq = sb("zq", [P, S], U32)
+        zs = sb("zs", [P, S], U8)
+        a_bank = {}
+        awin = [sb(f"awin{t}", [P, S], F32) for t in range(PACK)]
+        for h in range(HALVES):
+            zf = sb(f"zf{h}", [P, PACK, HALF], F32)
+            for t in range(PACK):
+                nc.vector.tensor_tensor(zf[:, t, :], ywin[t][:].indirect(half(l_n2, h)), absd[:, PACK - 1 - t, cols(h)], ALU.mult)
+            zb = sb(f"zb{h}", [P, PACK * HALF], BF16)
+            interleave(nc.vector.tensor_copy, zb[:], zf[:])
+            nc.vector.quantize_mx(out=zq[:, cols(h)].bitcast(FP8X4), scales=zs[:, cols(h)], in_=zb[:])
+            for tp in range(2):
+                a_bank[h, tp] = psum.tile([P, 2, HALF], F32, name=f"a_bank{h}{tp}", tag=f"ya{2 * h + tp}")
+                for u in range(2):
+                    mm_w(a_bank[h, tp][:, u, :], w3, w3s, 2 * tp + u, zq[:, cols(h)], zs[:, cols(h)])
+
+        for t in range(PACK):
+            for h in range(HALVES):
+                nc.scalar.activation(diff[:, h, t, :], lwin[t][:].indirect(half(l_n3, h)), ACT.Exp, scale=-1.0)
+        acopy = [sb(f"acopy{t}", [P, HALF], F32) for t in range(PACK)]
+        for h in range(HALVES):
+            for t in range(PACK):
+                nc.scalar.copy(awin[t][:, cols(h)], a_bank[h, t // 2][:, t % 2, :])
+        for t in range(PACK):
+            nc.sync.dma_start(acopy[t][:], awin[t][:, cols(0)])
+        z2p = sb("z2p", [P, PACK, S], BF16)
+        for t in range(PACK):
+            nc.vector.scalar_tensor_tensor(
+                z2p[:, t, :].rearrange("p (h n) -> p h n", h=HALVES),
+                d_bank[t][:].rearrange("p (h n) -> p h n", h=HALVES),
+                gs_t[:, t : t + 1],
+                diff[:, :, t, :],
+                ALU.mult,
+                ALU.mult,
+            )
+        z2q = sb("z2q", [P, S], U32)
+        z2s = sb("z2s", [P, S], U8)
+        b_bank = {}
+        z2b = [sb(f"z2b{h}", [P, PACK * HALF], BF16) for h in range(HALVES)]
+        for h in range(HALVES):
+            interleave(nc.vector.tensor_copy, z2b[h][:], z2p[:, :, cols(h)])
+        for h in range(HALVES):
+            nc.vector.quantize_mx(out=z2q[:, cols(h)].bitcast(FP8X4), scales=z2s[:, cols(h)], in_=z2b[h][:])
+            for tp in range(2):
+                b_bank[h, tp] = psum.tile([P, 2, HALF], F32, name=f"b_bank{h}{tp}", tag=f"db{2 * h + tp}")
+                for u in range(2):
+                    t = 2 * tp + u
+                    nc.tensor.matmul_mx(
+                        out=b_bank[h, tp][:, u, :],
+                        lhsT=cw[:, P * t : P * (t + 1)].bitcast(FP8X4),
+                        lhsT_scale=cs[:, P * t : P * (t + 1)],
+                        rhs=z2q[:, cols(h)].bitcast(FP8X4),
+                        rhs_scale=z2s[:, cols(h)],
+                        start=True,
+                        stop=True,
+                    )
+
+        a4 = [sb(f"a4_{h}", [P, PACK, HALF], F32) for h in range(HALVES)]
+        p5 = [sb(f"p5_{h}", [P, PACK, HALF], F32) for h in range(HALVES)]
+        b6 = [sb(f"b6_{h}", [P, PACK, HALF], F32) for h in range(HALVES)]
+        bwin = [sb(f"bwin{t}", [P, S], F32) for t in range(PACK)]
+
+        def gather_a4(h):
+            for t in range(PACK):
+                nc.scalar.activation(a4[h][:, t, :], awin[t][:].indirect(half(l_n4, h)), ACT.Copy)
+
+        def gather_b6(h):
+            for t in range(PACK):
+                nc.scalar.activation(b6[h][:, t, :], bwin[t][:].indirect(half(l_n6, h)), ACT.Copy)
+
+        gather_a4(0)
+        for t in range(PACK):
+            nc.vector.tensor_tensor(p5[0][:, t, :], awin[t][:].indirect(half(l_n5, 0)), acopy[t][:], ALU.subtract)
+        a5 = sb("a5", [P, PACK, HALF], F32)
+        gather_a4(1)
+        for t in range(PACK):
+            nc.scalar.activation(a5[:, t, :], awin[t][:].indirect(half(l_n5, 1)), ACT.Copy)
+        for h in range(HALVES):
+            for t in range(PACK):
+                nc.scalar.activation(bwin[t][:, cols(h)], b_bank[h, t // 2][:, t % 2, :], ACT.Copy, scale=0.03125)
+        gather_b6(0)
+        gather_b6(1)
+
+        oq = sb("oq", [P, S], U32)
+        osc = sb("osc", [P, S], U8)
+        out_rows = out_0.rearrange("(p t) n -> p t n", t=PACK)
+        out_words = out_1[0].rearrange("p n r -> p (n r)").bitcast(I32)
+        res, ob = [], []
+        for h in range(HALVES):
+            p4 = sb(f"p4_{h}", [P, PACK, HALF], F32)
+            t4 = sb(f"t4_{h}", [P, PACK, HALF], F32)
+            q5 = sb(f"q5_{h}", [P, PACK, HALF], F32)
+            res.append(sb(f"res{h}", [P, PACK, HALF], F32))
+            ob.append(sb(f"ob{h}", [P, PACK * HALF], BF16))
+            for tp in range(2):
+                pair = slice(2 * tp, 2 * tp + 2)
+                nc.vector.tensor_tensor(p4[:, pair, :], a4[h][:, pair, :], a_bank[h, tp][:], ALU.subtract)
+            if h == 1:
+                for tp in range(2):
+                    pair = slice(2 * tp, 2 * tp + 2)
+                    nc.vector.tensor_tensor(p5[h][:, pair, :], a5[:, pair, :], a_bank[h, tp][:], ALU.subtract)
+            for tp in range(2):
+                pair = slice(2 * tp, 2 * tp + 2)
+                nc.vector.scalar_tensor_tensor(t4[:, pair, :], b_bank[h, tp][:], 0.0625, p4[:, pair, :], ALU.mult, ALU.mult)
+            nc.vector.tensor_tensor(q5[:], b6[h][:], p5[h][:], ALU.mult)
+            nc.vector.tensor_tensor(res[h][:], t4[:], q5[:], ALU.add)
+            nc.sync.dma_start(out_rows[:, :, cols(h)], res[h][:])
+            interleave(nc.scalar.copy if h == 0 else nc.vector.tensor_copy, ob[h][:], res[h][:])
+        for h in range(HALVES):
+            nc.vector.quantize_mx(out=oq[:, cols(h)].bitcast(FP8X4), scales=osc[:, cols(h)], in_=ob[h][:])
+            nc.sync.dma_start(out_words[:, cols(h)], oq[:, cols(h)].bitcast(I32))
+        for q in range(4):
+            queue = nc.scalar if q % 2 else nc.sync
+            queue.dma_start(out_2[0, 4 * q : 4 * q + 4, :].bitcast(I32), osc[32 * q : 32 * q + 4, :].bitcast(I32))

@@ -20,6 +20,7 @@ S = 512
 HALF = 256
 HALVES = S // HALF
 LCOLS = HALF // 16
+FUSED = 3
 FLOPS = 4 * 2 * 512 * 512 * 512
 
 
@@ -55,30 +56,33 @@ def tile_picked_tfcdflowbfdifnorm_none_po_kernel(
         def cols(h):
             return slice(h * HALF, (h + 1) * HALF)
 
+        warm = sb("warm", [P, 2], F32)
+        nc.gpsimd.memset(warm[:, 0:1], 1.0)
+        nc.scalar.activation(warm[:, 1:2], warm[:, 0:1], ACT.Ln)
         xs = sb("xs", [P, T], U8)
         nc.gpsimd.memset(xs[:].bitcast(I32), 0)
         wsraw = [sb(f"wsraw{i}", [P, S], U8) for i in range(3)]
         for i in range(3):
             nc.gpsimd.memset(wsraw[i][:].bitcast(I32), 0)
-        load_scale_rows(nc.scalar, xs, x_scales)
         l_offs = load_list("l_offs", offs)
+        l_two = load_list("l_two", two)
+        load_scale_rows(nc.sync, xs, x_scales)
         xw = sb("xw", [P, T], I32)
         nc.sync.dma_start(xw[:], x_words[0].rearrange("p n t -> p (n t)").bitcast(I32))
         w1raw = load_w_words("w1raw", w1_words)
         load_scale_rows(nc.sync, wsraw[0], w1_scales)
-        l_two = load_list("l_two", two)
         gn_t = sb("gn_t", [P, PACK], F32)
         nc.sync.dma_start(gn_t[:], gn.rearrange("(p t) o -> p (t o)", t=PACK))
         w2raw = load_w_words("w2raw", w2_words)
-        load_scale_rows(nc.gpsimd, wsraw[1], w2_scales)
-        l_n1 = load_list("l_n1", n1)
+        load_scale_rows(nc.sync, wsraw[1], w2_scales)
         w3raw = load_w_words("w3raw", w3_words)
-        load_scale_rows(nc.sync, wsraw[2], w3_scales)
+        l_n1 = load_list("l_n1", n1)
+        l_cand = load_list("l_cand", cand)
         l_n2 = load_list("l_n2", n2)
         l_n3 = load_list("l_n3", n3)
         gs_t = sb("gs_t", [P, PACK], F32)
         nc.sync.dma_start(gs_t[:], gs.rearrange("(p t) o -> p (t o)", t=PACK))
-        l_cand = load_list("l_cand", cand)
+        load_scale_rows(nc.sync, wsraw[2], w3_scales)
         l_n4 = load_list("l_n4", n4)
         l_n5 = load_list("l_n5", n5)
         l_n6 = load_list("l_n6", n6)
@@ -110,15 +114,13 @@ def tile_picked_tfcdflowbfdifnorm_none_po_kernel(
             return tile
 
         xs_offs = gather_scales("xs_offs", l_offs)
-        xw_offs = gather_words("xw_offs", l_offs)
         xs_two = gather_scales("xs_two", l_two)
+        xw_offs = gather_words("xw_offs", l_offs)
         xw_two = gather_words("xw_two", l_two)
         w1 = deal_words("w1", w1raw)
-        w1s = deal(nc.vector, "w1s", wsraw[0], U8)
+        w1s = deal(nc.gpsimd, "w1s", wsraw[0], U8)
         w2 = deal_words("w2", w2raw)
         w2s = deal(nc.gpsimd, "w2s", wsraw[1], U8)
-        w3 = deal_words("w3", w3raw)
-        w3s = deal(nc.gpsimd, "w3s", wsraw[2], U8)
 
         gn_safe = sb("gn_safe", [P, PACK], F32)
         nc.vector.scalar_tensor_tensor(gn_safe[:], gn_t[:], 0.0, gn_t[:], ALU.is_equal, ALU.add)
@@ -136,27 +138,27 @@ def tile_picked_tfcdflowbfdifnorm_none_po_kernel(
                 stop=True,
             )
 
-        ywin = [sb(f"ywin{t}", [P, S], F32) for t in range(PACK)]
-        ycopy = [sb(f"ycopy{t}", [P, S], F32) for t in range(PACK)]
+        win_ya = [sb(f"win_ya{t}", [P, 2 * S], F32) for t in range(PACK)]
+        win_db = [sb(f"win_db{t}", [P, 2 * S], F32) for t in range(PACK)]
+        ycopy = [win_ya[(t - 1) % PACK][:, S:] for t in range(PACK)]
+        absd = [win_db[PACK - 1 - t][:, S:] for t in range(PACK)]
+        th = [win_db[t][:, S:] for t in range(PACK)]
         for t in range(PACK):
             bank = psum.tile([P, S], F32, name=f"y_bank{t}", tag=f"ya{t}")
             mm_w(bank[:], w1, w1s, t, xw_offs[:], xs_offs[:])
-            if t < 2:
-                nc.scalar.activation(ywin[t][:], bank[:], ACT.Copy, scale=gn_t[:, t : t + 1])
-            else:
-                nc.vector.tensor_scalar(ywin[t][:], bank[:], gn_t[:, t : t + 1], None, ALU.mult)
-            nc.sync.dma_start(ycopy[t][:], ywin[t][:])
+            nc.scalar.activation(win_ya[t][:, :S], bank[:], ACT.Copy, scale=gn_t[:, t : t + 1])
+            nc.gpsimd.tensor_scalar(ycopy[t], win_ya[t][:, :S], 1.0, 0.0, ALU.mult, ALU.add)
         d_bank = []
-        absd = sb("absd", [P, PACK, S], F32)
         for t in range(PACK):
             bank = psum.tile([P, S], F32, name=f"d_bank{t}", tag=f"db{t}")
             mm_w(bank[:], w2, w2s, t, xw_two[:], xs_two[:])
-            nc.scalar.activation(absd[:, t, :], bank[:], ACT.Abs)
+            nc.scalar.activation(absd[t], bank[:], ACT.Abs)
             d_bank.append(bank)
-        lwin = [sb(f"lwin{t}", [P, S], F32) for t in range(PACK)]
         for t in range(PACK):
-            nc.scalar.activation(lwin[t][:], absd[:, t, :], ACT.Ln, bias=0.5)
+            nc.scalar.activation(win_db[t][:, :S], absd[t], ACT.Ln, bias=0.5)
 
+        w3 = deal_words("w3", w3raw)
+        w3s = deal(nc.gpsimd, "w3s", wsraw[2], U8)
         xs_cand = gather_scales("xs_cand", l_cand)
         xw_cand = gather_words("xw_cand", l_cand)
         cw = deal(nc.vector, "cw", xw_cand, U32)
@@ -168,119 +170,91 @@ def tile_picked_tfcdflowbfdifnorm_none_po_kernel(
                 src.rearrange("p t (c i) -> p c t i", i=4),
             )
 
-        diff = sb("diff", [P, HALVES, PACK, HALF], F32)
-        for h in range(HALVES):
-            for t in range(PACK):
-                nc.vector.tensor_tensor(diff[:, h, t, :], ywin[t][:].indirect(half(l_n1, h)), ycopy[t][:, cols(h)], ALU.subtract)
-        for h in range(HALVES):
-            for t in range(PACK):
-                nc.scalar.activation(absd[:, PACK - 1 - t, cols(h)], diff[:, h, t, :], ACT.Tanh, scale=gn_inv[:, t : t + 1])
+        diff = sb("diff", [P, PACK, S], F32)
+        for t in range(PACK):
+            nc.vector.tensor_tensor(diff[:, t, :], win_ya[t][:].indirect(l_n1[:]), ycopy[t], ALU.subtract)
+        for t in range(PACK):
+            nc.scalar.activation(th[t], diff[:, t, :], ACT.Tanh, scale=gn_inv[:, t : t + 1])
+        zf = sb("zf", [P, PACK, S], F32)
+        for t in range(PACK):
+            nc.vector.tensor_tensor(zf[:, t, :], win_ya[t][:].indirect(l_n2[:]), th[t], ALU.mult)
+        zb = sb("zb", [P, PACK * S], BF16)
+        interleave(nc.vector.tensor_copy, zb[:], zf[:])
+        for t in range(PACK):
+            nc.scalar.activation(diff[:, t, :], win_db[t][:].indirect(l_n3[:]), ACT.Exp, scale=-1.0)
+        z2p = sb("z2p", [P, PACK, S], BF16)
+
+        def z2_plane(t):
+            nc.vector.scalar_tensor_tensor(z2p[:, t, :], d_bank[t][:], gs_t[:, t : t + 1], diff[:, t, :], ALU.mult, ALU.mult)
+
+        z2_plane(0)
         zq = sb("zq", [P, S], U32)
         zs = sb("zs", [P, S], U8)
-        a_bank = {}
-        awin = [sb(f"awin{t}", [P, S], F32) for t in range(PACK)]
-        for h in range(HALVES):
-            zf = sb(f"zf{h}", [P, PACK, HALF], F32)
-            for t in range(PACK):
-                nc.vector.tensor_tensor(zf[:, t, :], ywin[t][:].indirect(half(l_n2, h)), absd[:, PACK - 1 - t, cols(h)], ALU.mult)
-            zb = sb(f"zb{h}", [P, PACK * HALF], BF16)
-            interleave(nc.vector.tensor_copy, zb[:], zf[:])
-            nc.vector.quantize_mx(out=zq[:, cols(h)].bitcast(FP8X4), scales=zs[:, cols(h)], in_=zb[:])
-            for tp in range(2):
-                a_bank[h, tp] = psum.tile([P, 2, HALF], F32, name=f"a_bank{h}{tp}", tag=f"ya{2 * h + tp}")
-                for u in range(2):
-                    mm_w(a_bank[h, tp][:, u, :], w3, w3s, 2 * tp + u, zq[:, cols(h)], zs[:, cols(h)])
+        nc.vector.quantize_mx(out=zq[:].bitcast(FP8X4), scales=zs[:], in_=zb[:])
+        a_bank = []
+        acopy = [sb(f"acopy{t}", [P, S], F32) for t in range(FUSED)]
+        for t in range(PACK):
+            a_bank.append(psum.tile([P, S], F32, name=f"a_bank{t}", tag=f"ya{t}"))
+            mm_w(a_bank[t][:], w3, w3s, t, zq[:], zs[:])
+            nc.scalar.copy(win_ya[t][:, :S], a_bank[t][:])
+            if t < FUSED:
+                nc.sync.dma_start(acopy[t][:], win_ya[t][:, :S])
 
-        for t in range(PACK):
-            for h in range(HALVES):
-                nc.scalar.activation(diff[:, h, t, :], lwin[t][:].indirect(half(l_n3, h)), ACT.Exp, scale=-1.0)
-        acopy = [sb(f"acopy{t}", [P, HALF], F32) for t in range(PACK)]
-        for h in range(HALVES):
-            for t in range(PACK):
-                nc.scalar.copy(awin[t][:, cols(h)], a_bank[h, t // 2][:, t % 2, :])
-        for t in range(PACK):
-            nc.sync.dma_start(acopy[t][:], awin[t][:, cols(0)])
-        z2p = sb("z2p", [P, PACK, S], BF16)
-        for t in range(PACK):
-            nc.vector.scalar_tensor_tensor(
-                z2p[:, t, :].rearrange("p (h n) -> p h n", h=HALVES),
-                d_bank[t][:].rearrange("p (h n) -> p h n", h=HALVES),
-                gs_t[:, t : t + 1],
-                diff[:, :, t, :],
-                ALU.mult,
-                ALU.mult,
-            )
+        for t in range(1, PACK):
+            z2_plane(t)
+        z2b = sb("z2b", [P, PACK * S], BF16)
+        interleave(nc.vector.tensor_copy, z2b[:], z2p[:])
         z2q = sb("z2q", [P, S], U32)
         z2s = sb("z2s", [P, S], U8)
-        b_bank = {}
-        z2b = [sb(f"z2b{h}", [P, PACK * HALF], BF16) for h in range(HALVES)]
-        for h in range(HALVES):
-            interleave(nc.vector.tensor_copy, z2b[h][:], z2p[:, :, cols(h)])
-        for h in range(HALVES):
-            nc.vector.quantize_mx(out=z2q[:, cols(h)].bitcast(FP8X4), scales=z2s[:, cols(h)], in_=z2b[h][:])
-            for tp in range(2):
-                b_bank[h, tp] = psum.tile([P, 2, HALF], F32, name=f"b_bank{h}{tp}", tag=f"db{2 * h + tp}")
-                for u in range(2):
-                    t = 2 * tp + u
-                    nc.tensor.matmul_mx(
-                        out=b_bank[h, tp][:, u, :],
-                        lhsT=cw[:, P * t : P * (t + 1)].bitcast(FP8X4),
-                        lhsT_scale=cs[:, P * t : P * (t + 1)],
-                        rhs=z2q[:, cols(h)].bitcast(FP8X4),
-                        rhs_scale=z2s[:, cols(h)],
-                        start=True,
-                        stop=True,
-                    )
+        nc.vector.quantize_mx(out=z2q[:].bitcast(FP8X4), scales=z2s[:], in_=z2b[:])
+        b_bank = []
+        for t in range(PACK):
+            b_bank.append(psum.tile([P, S], F32, name=f"b_bank{t}", tag=f"db{t}"))
+            nc.tensor.matmul_mx(
+                out=b_bank[t][:],
+                lhsT=cw[:, P * t : P * (t + 1)].bitcast(FP8X4),
+                lhsT_scale=cs[:, P * t : P * (t + 1)],
+                rhs=z2q[:].bitcast(FP8X4),
+                rhs_scale=z2s[:],
+                start=True,
+                stop=True,
+            )
 
-        a4 = [sb(f"a4_{h}", [P, PACK, HALF], F32) for h in range(HALVES)]
-        p5 = [sb(f"p5_{h}", [P, PACK, HALF], F32) for h in range(HALVES)]
+        a4 = sb("a4", [P, PACK, S], F32)
+        a5 = sb("a5", [P, PACK - FUSED, S], F32)
+        p4 = sb("p4", [P, PACK, S], F32)
+        p5 = sb("p5", [P, PACK, S], F32)
+        t4 = sb("t4", [P, PACK, S], F32)
         b6 = [sb(f"b6_{h}", [P, PACK, HALF], F32) for h in range(HALVES)]
-        bwin = [sb(f"bwin{t}", [P, S], F32) for t in range(PACK)]
-
-        def gather_a4(h):
-            for t in range(PACK):
-                nc.scalar.activation(a4[h][:, t, :], awin[t][:].indirect(half(l_n4, h)), ACT.Copy)
-
-        def gather_b6(h):
-            for t in range(PACK):
-                nc.scalar.activation(b6[h][:, t, :], bwin[t][:].indirect(half(l_n6, h)), ACT.Copy)
-
-        gather_a4(0)
         for t in range(PACK):
-            nc.vector.tensor_tensor(p5[0][:, t, :], awin[t][:].indirect(half(l_n5, 0)), acopy[t][:], ALU.subtract)
-        a5 = sb("a5", [P, PACK, HALF], F32)
-        gather_a4(1)
+            nc.scalar.activation(a4[:, t, :], win_ya[t][:].indirect(l_n4[:]), ACT.Copy)
+        for t in range(FUSED, PACK):
+            nc.scalar.activation(a5[:, t - FUSED, :], win_ya[t][:].indirect(l_n5[:]), ACT.Copy)
+        for t in range(FUSED):
+            nc.vector.tensor_tensor(p5[:, t, :], win_ya[t][:].indirect(l_n5[:]), acopy[t][:], ALU.subtract)
         for t in range(PACK):
-            nc.scalar.activation(a5[:, t, :], awin[t][:].indirect(half(l_n5, 1)), ACT.Copy)
+            nc.vector.tensor_tensor(p4[:, t, :], a4[:, t, :], a_bank[t][:], ALU.subtract)
+        for t in range(FUSED, PACK):
+            nc.vector.tensor_tensor(p5[:, t, :], a5[:, t - FUSED, :], a_bank[t][:], ALU.subtract)
+        for t in range(PACK):
+            nc.scalar.activation(win_db[t][:, :S], b_bank[t][:], ACT.Copy, scale=0.03125)
+        for t in range(PACK):
+            nc.vector.scalar_tensor_tensor(t4[:, t, :], b_bank[t][:], 0.0625, p4[:, t, :], ALU.mult, ALU.mult)
         for h in range(HALVES):
             for t in range(PACK):
-                nc.scalar.activation(bwin[t][:, cols(h)], b_bank[h, t // 2][:, t % 2, :], ACT.Copy, scale=0.03125)
-        gather_b6(0)
-        gather_b6(1)
+                nc.scalar.activation(b6[h][:, t, :], win_db[t][:].indirect(half(l_n6, h)), ACT.Copy)
 
         oq = sb("oq", [P, S], U32)
         osc = sb("osc", [P, S], U8)
         out_rows = out_0.rearrange("(p t) n -> p t n", t=PACK)
         out_words = out_1[0].rearrange("p n r -> p (n r)").bitcast(I32)
         res, ob = [], []
+        q5 = sb("q5", [P, PACK, HALF], F32)
         for h in range(HALVES):
-            p4 = sb(f"p4_{h}", [P, PACK, HALF], F32)
-            t4 = sb(f"t4_{h}", [P, PACK, HALF], F32)
-            q5 = sb(f"q5_{h}", [P, PACK, HALF], F32)
             res.append(sb(f"res{h}", [P, PACK, HALF], F32))
             ob.append(sb(f"ob{h}", [P, PACK * HALF], BF16))
-            for tp in range(2):
-                pair = slice(2 * tp, 2 * tp + 2)
-                nc.vector.tensor_tensor(p4[:, pair, :], a4[h][:, pair, :], a_bank[h, tp][:], ALU.subtract)
-            if h == 1:
-                for tp in range(2):
-                    pair = slice(2 * tp, 2 * tp + 2)
-                    nc.vector.tensor_tensor(p5[h][:, pair, :], a5[:, pair, :], a_bank[h, tp][:], ALU.subtract)
-            for tp in range(2):
-                pair = slice(2 * tp, 2 * tp + 2)
-                nc.vector.scalar_tensor_tensor(t4[:, pair, :], b_bank[h, tp][:], 0.0625, p4[:, pair, :], ALU.mult, ALU.mult)
-            nc.vector.tensor_tensor(q5[:], b6[h][:], p5[h][:], ALU.mult)
-            nc.vector.tensor_tensor(res[h][:], t4[:], q5[:], ALU.add)
+            nc.vector.tensor_tensor(q5[:], b6[h][:], p5[:, :, cols(h)], ALU.mult)
+            nc.vector.tensor_tensor(res[h][:], t4[:, :, cols(h)], q5[:], ALU.add)
             nc.sync.dma_start(out_rows[:, :, cols(h)], res[h][:])
             interleave(nc.scalar.copy if h == 0 else nc.vector.tensor_copy, ob[h][:], res[h][:])
         for h in range(HALVES):

@@ -14,14 +14,17 @@ ALU = mybir.AluOpType
 ACT = mybir.ActivationFunctionType
 
 P = 128
-PACK = 4
+PLANES = 4
+QUADRANTS = 4
 T = 2048
 S = 512
+GROUP = 16
 HALF = 256
 HALVES = S // HALF
-LCOLS = HALF // 16
-FUSED = 3
-FLOPS = 4 * 2 * 512 * 512 * 512
+RUN = 4
+Y_ON_SCALAR = 3
+N5_ON_VECTOR = 3
+FLOPS = 4 * 2 * S * S * S
 
 
 def tile_picked_tfcdflowbfdifnorm_none_po_kernel(
@@ -36,53 +39,54 @@ def tile_picked_tfcdflowbfdifnorm_none_po_kernel(
         def sb(name, shape, dtype):
             return keep.tile(shape, dtype, name=name, align_bytes=64)
 
+        def cols(h):
+            return slice(h * HALF, (h + 1) * HALF)
+
         def load_list(name, src):
-            tile = keep.tile([P, S // 16], U16, name=name)
+            tile = keep.tile([P, S // GROUP], U16, name=name)
             nc.sync.dma_start(tile[:], src)
             return tile
 
-        def load_scale_rows(queue, tile, src):
-            for q in range(4):
-                queue.dma_start(tile[32 * q : 32 * q + 4, :].bitcast(I32), src[0, 4 * q : 4 * q + 4, :].bitcast(I32))
+        def load_scale_rows(tile, src):
+            for q in range(QUADRANTS):
+                nc.sync.dma_start(tile[32 * q : 32 * q + 4, :].bitcast(I32), src[0, 4 * q : 4 * q + 4, :].bitcast(I32))
 
         def load_w_words(name, src):
             tile = sb(name, [P, 2 * S], U8)
             nc.sync.dma_start(tile[:].bitcast(I32), src[0].bitcast(I32))
             return tile
 
-        def half(lst, h):
-            return lst[:, h * LCOLS : (h + 1) * LCOLS]
-
-        def cols(h):
-            return slice(h * HALF, (h + 1) * HALF)
+        def load_row_factor(name, src):
+            tile = sb(name, [P, PLANES], F32)
+            nc.sync.dma_start(tile[:], src.rearrange("(p t) o -> p (t o)", t=PLANES))
+            return tile
 
         warm = sb("warm", [P, 2], F32)
         nc.gpsimd.memset(warm[:, 0:1], 1.0)
         nc.scalar.activation(warm[:, 1:2], warm[:, 0:1], ACT.Ln)
+
         xs = sb("xs", [P, T], U8)
         nc.gpsimd.memset(xs[:].bitcast(I32), 0)
         wsraw = [sb(f"wsraw{i}", [P, S], U8) for i in range(3)]
-        for i in range(3):
-            nc.gpsimd.memset(wsraw[i][:].bitcast(I32), 0)
+        for tile in wsraw:
+            nc.gpsimd.memset(tile[:].bitcast(I32), 0)
         l_offs = load_list("l_offs", offs)
         l_two = load_list("l_two", two)
-        load_scale_rows(nc.sync, xs, x_scales)
+        load_scale_rows(xs, x_scales)
         xw = sb("xw", [P, T], I32)
         nc.sync.dma_start(xw[:], x_words[0].rearrange("p n t -> p (n t)").bitcast(I32))
         w1raw = load_w_words("w1raw", w1_words)
-        load_scale_rows(nc.sync, wsraw[0], w1_scales)
-        gn_t = sb("gn_t", [P, PACK], F32)
-        nc.sync.dma_start(gn_t[:], gn.rearrange("(p t) o -> p (t o)", t=PACK))
+        load_scale_rows(wsraw[0], w1_scales)
+        gn_t = load_row_factor("gn_t", gn)
         w2raw = load_w_words("w2raw", w2_words)
-        load_scale_rows(nc.sync, wsraw[1], w2_scales)
+        l_cand = load_list("l_cand", cand)
+        load_scale_rows(wsraw[1], w2_scales)
         w3raw = load_w_words("w3raw", w3_words)
         l_n1 = load_list("l_n1", n1)
-        l_cand = load_list("l_cand", cand)
         l_n2 = load_list("l_n2", n2)
         l_n3 = load_list("l_n3", n3)
-        gs_t = sb("gs_t", [P, PACK], F32)
-        nc.sync.dma_start(gs_t[:], gs.rearrange("(p t) o -> p (t o)", t=PACK))
-        load_scale_rows(nc.sync, wsraw[2], w3_scales)
+        gs_t = load_row_factor("gs_t", gs)
+        load_scale_rows(wsraw[2], w3_scales)
         l_n4 = load_list("l_n4", n4)
         l_n5 = load_list("l_n5", n5)
         l_n6 = load_list("l_n6", n6)
@@ -97,19 +101,19 @@ def tile_picked_tfcdflowbfdifnorm_none_po_kernel(
             nc.vector.tensor_copy(tile[:], xw[:].bitcast(U32).indirect(lst[:]))
             return tile
 
-        def deal_words(name, raw):
+        def deal_w_words(name, raw):
             tile = sb(name, [P, 2 * S], U8)
             nc.scalar.copy(
-                tile[:].bitcast(U16).rearrange("p (t m) -> p t m", t=PACK),
-                raw[:].bitcast(U16).rearrange("p (m t) -> p t m", t=PACK),
+                tile[:].bitcast(U16).rearrange("p (t m) -> p t m", t=PLANES),
+                raw[:].bitcast(U16).rearrange("p (m t) -> p t m", t=PLANES),
             )
             return tile
 
         def deal(engine, name, raw, dtype):
             tile = sb(name, [P, S], dtype)
             engine.tensor_copy(
-                tile[:].rearrange("p (t m) -> p t m", t=PACK),
-                raw[:].rearrange("p (m t) -> p t m", t=PACK),
+                tile[:].rearrange("p (t m) -> p t m", t=PLANES),
+                raw[:].rearrange("p (m t) -> p t m", t=PLANES),
             )
             return tile
 
@@ -117,149 +121,139 @@ def tile_picked_tfcdflowbfdifnorm_none_po_kernel(
         xs_two = gather_scales("xs_two", l_two)
         xw_offs = gather_words("xw_offs", l_offs)
         xw_two = gather_words("xw_two", l_two)
-        w1 = deal_words("w1", w1raw)
+        w1 = deal_w_words("w1", w1raw)
         w1s = deal(nc.gpsimd, "w1s", wsraw[0], U8)
-        w2 = deal_words("w2", w2raw)
+        w2 = deal_w_words("w2", w2raw)
         w2s = deal(nc.gpsimd, "w2s", wsraw[1], U8)
 
-        gn_safe = sb("gn_safe", [P, PACK], F32)
+        gn_safe = sb("gn_safe", [P, PLANES], F32)
         nc.vector.scalar_tensor_tensor(gn_safe[:], gn_t[:], 0.0, gn_t[:], ALU.is_equal, ALU.add)
-        gn_inv = sb("gn_inv", [P, PACK], F32)
+        gn_inv = sb("gn_inv", [P, PLANES], F32)
         nc.vector.reciprocal(gn_inv[:], gn_safe[:])
 
-        def mm_w(out, w, ws, t, xq, xq_s):
+        def product_plane(out, words, scales, t, rhs, rhs_scale):
             nc.tensor.matmul_mx(
                 out=out,
-                lhsT=w[:, 2 * P * t : 2 * P * (t + 1)].bitcast(FP4X4),
-                lhsT_scale=ws[:, P * t : P * (t + 1)],
-                rhs=xq.bitcast(FP8X4),
-                rhs_scale=xq_s,
+                lhsT=words[:, P * t : P * (t + 1)],
+                lhsT_scale=scales[:, P * t : P * (t + 1)],
+                rhs=rhs.bitcast(FP8X4),
+                rhs_scale=rhs_scale,
                 start=True,
                 stop=True,
             )
 
-        win_ya = [sb(f"win_ya{t}", [P, 2 * S], F32) for t in range(PACK)]
-        win_db = [sb(f"win_db{t}", [P, 2 * S], F32) for t in range(PACK)]
-        ycopy = [win_ya[(t - 1) % PACK][:, S:] for t in range(PACK)]
-        absd = [win_db[PACK - 1 - t][:, S:] for t in range(PACK)]
-        th = [win_db[t][:, S:] for t in range(PACK)]
-        for t in range(PACK):
-            bank = psum.tile([P, S], F32, name=f"y_bank{t}", tag=f"ya{t}")
-            mm_w(bank[:], w1, w1s, t, xw_offs[:], xs_offs[:])
-            nc.scalar.activation(win_ya[t][:, :S], bank[:], ACT.Copy, scale=gn_t[:, t : t + 1])
+        def interleave(copy, dst, src):
+            copy(
+                dst.rearrange("p (c i t) -> p c t i", i=RUN, t=PLANES),
+                src.rearrange("p t (c i) -> p c t i", i=RUN),
+            )
+
+        win_ya = [sb(f"win_ya{t}", [P, 2 * S], F32) for t in range(PLANES)]
+        win_db = [sb(f"win_db{t}", [P, 2 * S], F32) for t in range(PLANES)]
+        ycopy = [win_ya[(t - 1) % PLANES][:, S:] for t in range(PLANES)]
+        absd = [win_db[PLANES - 1 - t][:, S:] for t in range(PLANES)]
+        th = [win_db[t][:, S:] for t in range(PLANES)]
+        for t in range(PLANES):
+            y_bank = psum.tile([P, S], F32, name=f"y_bank{t}", tag=f"ya{t}")
+            product_plane(y_bank[:], w1[:].bitcast(FP4X4), w1s, t, xw_offs[:], xs_offs[:])
+            if t < Y_ON_SCALAR:
+                nc.scalar.activation(win_ya[t][:, :S], y_bank[:], ACT.Copy, scale=gn_t[:, t : t + 1])
+            else:
+                nc.vector.tensor_scalar(win_ya[t][:, :S], y_bank[:], gn_t[:, t : t + 1], None, ALU.mult)
             nc.gpsimd.tensor_scalar(ycopy[t], win_ya[t][:, :S], 1.0, 0.0, ALU.mult, ALU.add)
         d_bank = []
-        for t in range(PACK):
-            bank = psum.tile([P, S], F32, name=f"d_bank{t}", tag=f"db{t}")
-            mm_w(bank[:], w2, w2s, t, xw_two[:], xs_two[:])
-            nc.scalar.activation(absd[t], bank[:], ACT.Abs)
-            d_bank.append(bank)
-        for t in range(PACK):
+        for t in range(PLANES):
+            d_bank.append(psum.tile([P, S], F32, name=f"d_bank{t}", tag=f"db{t}"))
+            product_plane(d_bank[t][:], w2[:].bitcast(FP4X4), w2s, t, xw_two[:], xs_two[:])
+            nc.scalar.activation(absd[t], d_bank[t][:], ACT.Abs)
+        for t in range(PLANES):
             nc.scalar.activation(win_db[t][:, :S], absd[t], ACT.Ln, bias=0.5)
 
-        w3 = deal_words("w3", w3raw)
+        w3 = deal_w_words("w3", w3raw)
         w3s = deal(nc.gpsimd, "w3s", wsraw[2], U8)
         xs_cand = gather_scales("xs_cand", l_cand)
         xw_cand = gather_words("xw_cand", l_cand)
         cw = deal(nc.vector, "cw", xw_cand, U32)
         cs = deal(nc.vector, "cs", xs_cand, U8)
 
-        def interleave(engine_copy, dst, src):
-            engine_copy(
-                dst.rearrange("p (c i t) -> p c t i", i=4, t=PACK),
-                src.rearrange("p t (c i) -> p c t i", i=4),
-            )
-
-        diff = sb("diff", [P, PACK, S], F32)
-        for t in range(PACK):
-            nc.vector.tensor_tensor(diff[:, t, :], win_ya[t][:].indirect(l_n1[:]), ycopy[t], ALU.subtract)
-        for t in range(PACK):
-            nc.scalar.activation(th[t], diff[:, t, :], ACT.Tanh, scale=gn_inv[:, t : t + 1])
-        zf = sb("zf", [P, PACK, S], F32)
-        for t in range(PACK):
+        stage = sb("stage", [P, PLANES, S], F32)
+        for t in range(PLANES):
+            nc.vector.tensor_tensor(stage[:, t, :], win_ya[t][:].indirect(l_n1[:]), ycopy[t], ALU.subtract)
+        for t in range(PLANES):
+            nc.scalar.activation(th[t], stage[:, t, :], ACT.Tanh, scale=gn_inv[:, t : t + 1])
+        zf = sb("zf", [P, PLANES, S], F32)
+        for t in range(PLANES):
             nc.vector.tensor_tensor(zf[:, t, :], win_ya[t][:].indirect(l_n2[:]), th[t], ALU.mult)
-        zb = sb("zb", [P, PACK * S], BF16)
+        zb = sb("zb", [P, PLANES * S], BF16)
         interleave(nc.vector.tensor_copy, zb[:], zf[:])
-        for t in range(PACK):
-            nc.scalar.activation(diff[:, t, :], win_db[t][:].indirect(l_n3[:]), ACT.Exp, scale=-1.0)
-        z2p = sb("z2p", [P, PACK, S], BF16)
-
-        def z2_plane(t):
-            nc.vector.scalar_tensor_tensor(z2p[:, t, :], d_bank[t][:], gs_t[:, t : t + 1], diff[:, t, :], ALU.mult, ALU.mult)
-
-        z2_plane(0)
+        for t in range(PLANES):
+            nc.scalar.activation(stage[:, t, :], win_db[t][:].indirect(l_n3[:]), ACT.Exp, scale=-1.0)
         zq = sb("zq", [P, S], U32)
         zs = sb("zs", [P, S], U8)
         nc.vector.quantize_mx(out=zq[:].bitcast(FP8X4), scales=zs[:], in_=zb[:])
         a_bank = []
-        acopy = [sb(f"acopy{t}", [P, S], F32) for t in range(FUSED)]
-        for t in range(PACK):
+        acopy = [sb(f"acopy{t}", [P, S], F32) for t in range(N5_ON_VECTOR)]
+        for t in range(PLANES):
             a_bank.append(psum.tile([P, S], F32, name=f"a_bank{t}", tag=f"ya{t}"))
-            mm_w(a_bank[t][:], w3, w3s, t, zq[:], zs[:])
+            product_plane(a_bank[t][:], w3[:].bitcast(FP4X4), w3s, t, zq[:], zs[:])
             nc.scalar.copy(win_ya[t][:, :S], a_bank[t][:])
-            if t < FUSED:
+            if t < N5_ON_VECTOR:
                 nc.sync.dma_start(acopy[t][:], win_ya[t][:, :S])
 
-        for t in range(1, PACK):
-            z2_plane(t)
-        z2b = sb("z2b", [P, PACK * S], BF16)
-        interleave(nc.vector.tensor_copy, z2b[:], z2p[:])
+        z2p = zb[:].rearrange("p (t n) -> p t n", t=PLANES)
+        for t in range(PLANES):
+            nc.vector.scalar_tensor_tensor(z2p[:, t, :], d_bank[t][:], gs_t[:, t : t + 1], stage[:, t, :], ALU.mult, ALU.mult)
+        z2b = sb("z2b", [P, PLANES * S], BF16)
+        interleave(nc.vector.tensor_copy, z2b[:], z2p)
         z2q = sb("z2q", [P, S], U32)
         z2s = sb("z2s", [P, S], U8)
         nc.vector.quantize_mx(out=z2q[:].bitcast(FP8X4), scales=z2s[:], in_=z2b[:])
-        b_bank = []
-        for t in range(PACK):
-            b_bank.append(psum.tile([P, S], F32, name=f"b_bank{t}", tag=f"db{t}"))
-            nc.tensor.matmul_mx(
-                out=b_bank[t][:],
-                lhsT=cw[:, P * t : P * (t + 1)].bitcast(FP8X4),
-                lhsT_scale=cs[:, P * t : P * (t + 1)],
-                rhs=z2q[:].bitcast(FP8X4),
-                rhs_scale=z2s[:],
-                start=True,
-                stop=True,
-            )
+        b16_bank = []
+        for t in range(PLANES):
+            b16_bank.append(psum.tile([P, S], F32, name=f"b16_bank{t}", tag=f"db{t}"))
+            product_plane(b16_bank[t][:], cw[:].bitcast(FP8X4), cs, t, z2q[:], z2s[:])
 
-        a4 = sb("a4", [P, PACK, S], F32)
-        a5 = sb("a5", [P, PACK - FUSED, S], F32)
-        p4 = sb("p4", [P, PACK, S], F32)
-        p5 = sb("p5", [P, PACK, S], F32)
-        t4 = sb("t4", [P, PACK, S], F32)
-        b6 = [sb(f"b6_{h}", [P, PACK, HALF], F32) for h in range(HALVES)]
-        for t in range(PACK):
+        a4 = sb("a4", [P, PLANES, S], F32)
+        a5 = sb("a5", [P, PLANES - N5_ON_VECTOR, S], F32)
+        d4 = sb("d4", [P, PLANES, S], F32)
+        d5 = sb("d5", [P, PLANES, S], F32)
+        first = sb("first", [P, PLANES, S], F32)
+        b6 = [sb(f"b6_{h}", [P, PLANES, HALF], F32) for h in range(HALVES)]
+        for t in range(PLANES):
             nc.scalar.activation(a4[:, t, :], win_ya[t][:].indirect(l_n4[:]), ACT.Copy)
-        for t in range(FUSED, PACK):
-            nc.scalar.activation(a5[:, t - FUSED, :], win_ya[t][:].indirect(l_n5[:]), ACT.Copy)
-        for t in range(FUSED):
-            nc.vector.tensor_tensor(p5[:, t, :], win_ya[t][:].indirect(l_n5[:]), acopy[t][:], ALU.subtract)
-        for t in range(PACK):
-            nc.vector.tensor_tensor(p4[:, t, :], a4[:, t, :], a_bank[t][:], ALU.subtract)
-        for t in range(FUSED, PACK):
-            nc.vector.tensor_tensor(p5[:, t, :], a5[:, t - FUSED, :], a_bank[t][:], ALU.subtract)
-        for t in range(PACK):
-            nc.scalar.activation(win_db[t][:, :S], b_bank[t][:], ACT.Copy, scale=0.03125)
-        for t in range(PACK):
-            nc.vector.scalar_tensor_tensor(t4[:, t, :], b_bank[t][:], 0.0625, p4[:, t, :], ALU.mult, ALU.mult)
+        for t in range(N5_ON_VECTOR, PLANES):
+            nc.scalar.activation(a5[:, t - N5_ON_VECTOR, :], win_ya[t][:].indirect(l_n5[:]), ACT.Copy)
+        for t in range(N5_ON_VECTOR):
+            nc.vector.tensor_tensor(d5[:, t, :], win_ya[t][:].indirect(l_n5[:]), acopy[t][:], ALU.subtract)
+        for t in range(PLANES):
+            nc.vector.tensor_tensor(d4[:, t, :], a4[:, t, :], a_bank[t][:], ALU.subtract)
+        for t in range(N5_ON_VECTOR, PLANES):
+            nc.vector.tensor_tensor(d5[:, t, :], a5[:, t - N5_ON_VECTOR, :], a_bank[t][:], ALU.subtract)
+        for t in range(PLANES):
+            nc.scalar.activation(win_db[t][:, :S], b16_bank[t][:], ACT.Copy, scale=0.5 / 16)
+        for t in range(PLANES):
+            nc.vector.scalar_tensor_tensor(first[:, t, :], b16_bank[t][:], 1.0 / 16, d4[:, t, :], ALU.mult, ALU.mult)
         for h in range(HALVES):
-            for t in range(PACK):
-                nc.scalar.activation(b6[h][:, t, :], win_db[t][:].indirect(half(l_n6, h)), ACT.Copy)
+            n6_half = l_n6[:, h * HALF // GROUP : (h + 1) * HALF // GROUP]
+            for t in range(PLANES):
+                nc.scalar.activation(b6[h][:, t, :], win_db[t][:].indirect(n6_half), ACT.Copy)
 
         oq = sb("oq", [P, S], U32)
         osc = sb("osc", [P, S], U8)
-        out_rows = out_0.rearrange("(p t) n -> p t n", t=PACK)
+        out_rows = out_0.rearrange("(p t) n -> p t n", t=PLANES)
         out_words = out_1[0].rearrange("p n r -> p (n r)").bitcast(I32)
-        res, ob = [], []
-        q5 = sb("q5", [P, PACK, HALF], F32)
+        second = sb("second", [P, PLANES, HALF], F32)
+        ob = []
         for h in range(HALVES):
-            res.append(sb(f"res{h}", [P, PACK, HALF], F32))
-            ob.append(sb(f"ob{h}", [P, PACK * HALF], BF16))
-            nc.vector.tensor_tensor(q5[:], b6[h][:], p5[:, :, cols(h)], ALU.mult)
-            nc.vector.tensor_tensor(res[h][:], t4[:, :, cols(h)], q5[:], ALU.add)
-            nc.sync.dma_start(out_rows[:, :, cols(h)], res[h][:])
-            interleave(nc.scalar.copy if h == 0 else nc.vector.tensor_copy, ob[h][:], res[h][:])
+            res = sb(f"res{h}", [P, PLANES, HALF], F32)
+            ob.append(sb(f"ob{h}", [P, PLANES * HALF], BF16))
+            nc.vector.tensor_tensor(second[:], b6[h][:], d5[:, :, cols(h)], ALU.mult)
+            nc.vector.tensor_tensor(res[:], first[:, :, cols(h)], second[:], ALU.add)
+            nc.sync.dma_start(out_rows[:, :, cols(h)], res[:])
+            interleave(nc.vector.tensor_copy if h == HALVES - 1 else nc.scalar.copy, ob[h][:], res[:])
         for h in range(HALVES):
             nc.vector.quantize_mx(out=oq[:, cols(h)].bitcast(FP8X4), scales=osc[:, cols(h)], in_=ob[h][:])
             nc.sync.dma_start(out_words[:, cols(h)], oq[:, cols(h)].bitcast(I32))
-        for q in range(4):
+        for q in range(QUADRANTS):
             queue = nc.scalar if q % 2 else nc.sync
             queue.dma_start(out_2[0, 4 * q : 4 * q + 4, :].bitcast(I32), osc[32 * q : 32 * q + 4, :].bitcast(I32))

from contextlib import ExitStack

import concourse.mybir as mybir

F32 = mybir.dt.float32
BF16 = mybir.dt.bfloat16
I32 = mybir.dt.int32
U32 = mybir.dt.uint32
U16 = mybir.dt.uint16
U8 = mybir.dt.uint8
FP8X4 = mybir.dt.float8_e4m3fn_x4
FP4X4 = mybir.dt.float4_e2m1fn_x4
ALU = mybir.AluOpType
ACT = mybir.ActivationFunctionType

P = 128
PLANES = 4
QUADRANTS = 4
T = 2048
S = 512
GROUP = 16
HALF = 256
HALVES = S // HALF
RUN = 4
Y_ON_SCALAR = 3
N5_ON_VECTOR = 3
FLOPS = 4 * 2 * S * S * S


def tile_picked_tfcdflowbfdifnorm_none_po_kernel(
    tc, x_words, x_scales, w1_words, w1_scales, w2_words, w2_scales, gn, w3_words, w3_scales, gs,
    offs, two, n1, n2, n3, cand, n4, n5, n6, out_0, out_1, out_2,
):
    nc = tc.nc
    with ExitStack() as ctx:
        keep = ctx.enter_context(tc.tile_pool(name="keep", bufs=1))
        psum = ctx.enter_context(tc.psum_pool(name="psum", bufs=1))

        def sb(name, shape, dtype):
            return keep.tile(shape, dtype, name=name, align_bytes=64)

        def cols(h):
            return slice(h * HALF, (h + 1) * HALF)

        def load_list(name, src):
            tile = keep.tile([P, S // GROUP], U16, name=name)
            nc.sync.dma_start(tile[:], src)
            return tile

        def load_scale_rows(tile, src):
            for q in range(QUADRANTS):
                nc.sync.dma_start(tile[32 * q : 32 * q + 4, :].bitcast(I32), src[0, 4 * q : 4 * q + 4, :].bitcast(I32))

        def load_w_words(name, src):
            tile = sb(name, [P, 2 * S], U8)
            nc.sync.dma_start(tile[:].bitcast(I32), src[0].bitcast(I32))
            return tile

        def load_row_factor(name, src):
            tile = sb(name, [P, PLANES], F32)
            nc.sync.dma_start(tile[:], src.rearrange("(p t) o -> p (t o)", t=PLANES))
            return tile

        warm = sb("warm", [P, 2], F32)
        nc.gpsimd.memset(warm[:, 0:1], 1.0)
        nc.scalar.activation(warm[:, 1:2], warm[:, 0:1], ACT.Ln)

        xs = sb("xs", [P, T], U8)
        nc.gpsimd.memset(xs[:].bitcast(I32), 0)
        wsraw = [sb(f"wsraw{i}", [P, S], U8) for i in range(3)]
        for tile in wsraw:
            nc.gpsimd.memset(tile[:].bitcast(I32), 0)
        l_offs = load_list("l_offs", offs)
        l_two = load_list("l_two", two)
        load_scale_rows(xs, x_scales)
        xw = sb("xw", [P, T], I32)
        nc.sync.dma_start(xw[:], x_words[0].rearrange("p n t -> p (n t)").bitcast(I32))
        w1raw = load_w_words("w1raw", w1_words)
        load_scale_rows(wsraw[0], w1_scales)
        gn_t = load_row_factor("gn_t", gn)
        w2raw = load_w_words("w2raw", w2_words)
        l_cand = load_list("l_cand", cand)
        load_scale_rows(wsraw[1], w2_scales)
        w3raw = load_w_words("w3raw", w3_words)
        l_n1 = load_list("l_n1", n1)
        l_n2 = load_list("l_n2", n2)
        l_n3 = load_list("l_n3", n3)
        gs_t = load_row_factor("gs_t", gs)
        load_scale_rows(wsraw[2], w3_scales)
        l_n4 = load_list("l_n4", n4)
        l_n5 = load_list("l_n5", n5)
        l_n6 = load_list("l_n6", n6)

        def gather_scales(name, lst):
            tile = sb(name, [P, S], U8)
            nc.vector.tensor_copy(tile[:], xs[:].indirect(lst[:]))
            return tile

        def gather_words(name, lst):
            tile = sb(name, [P, S], U32)
            nc.vector.tensor_copy(tile[:], xw[:].bitcast(U32).indirect(lst[:]))
            return tile

        def deal_w_words(name, raw):
            tile = sb(name, [P, 2 * S], U8)
            nc.scalar.copy(
                tile[:].bitcast(U16).rearrange("p (t m) -> p t m", t=PLANES),
                raw[:].bitcast(U16).rearrange("p (m t) -> p t m", t=PLANES),
            )
            return tile

        def deal(engine, name, raw, dtype):
            tile = sb(name, [P, S], dtype)
            engine.tensor_copy(
                tile[:].rearrange("p (t m) -> p t m", t=PLANES),
                raw[:].rearrange("p (m t) -> p t m", t=PLANES),
            )
            return tile

        xs_offs = gather_scales("xs_offs", l_offs)
        xs_two = gather_scales("xs_two", l_two)
        xw_offs = gather_words("xw_offs", l_offs)
        xw_two = gather_words("xw_two", l_two)
        w1 = deal_w_words("w1", w1raw)
        w1s = deal(nc.gpsimd, "w1s", wsraw[0], U8)
        w2 = deal_w_words("w2", w2raw)
        w2s = deal(nc.gpsimd, "w2s", wsraw[1], U8)

        gn_safe = sb("gn_safe", [P, PLANES], F32)
        nc.vector.scalar_tensor_tensor(gn_safe[:], gn_t[:], 0.0, gn_t[:], ALU.is_equal, ALU.add)
        gn_inv = sb("gn_inv", [P, PLANES], F32)
        nc.vector.reciprocal(gn_inv[:], gn_safe[:])

        def product_plane(out, words, scales, t, rhs, rhs_scale):
            nc.tensor.matmul_mx(
                out=out,
                lhsT=words[:, P * t : P * (t + 1)],
                lhsT_scale=scales[:, P * t : P * (t + 1)],
                rhs=rhs.bitcast(FP8X4),
                rhs_scale=rhs_scale,
                start=True,
                stop=True,
            )

        def interleave(copy, dst, src):
            copy(
                dst.rearrange("p (c i t) -> p c t i", i=RUN, t=PLANES),
                src.rearrange("p t (c i) -> p c t i", i=RUN),
            )

        win_ya = [sb(f"win_ya{t}", [P, 2 * S], F32) for t in range(PLANES)]
        win_db = [sb(f"win_db{t}", [P, 2 * S], F32) for t in range(PLANES)]
        ycopy = [win_ya[(t - 1) % PLANES][:, S:] for t in range(PLANES)]
        absd = [win_db[PLANES - 1 - t][:, S:] for t in range(PLANES)]
        th = [win_db[t][:, S:] for t in range(PLANES)]
        for t in range(PLANES):
            y_bank = psum.tile([P, S], F32, name=f"y_bank{t}", tag=f"ya{t}")
            product_plane(y_bank[:], w1[:].bitcast(FP4X4), w1s, t, xw_offs[:], xs_offs[:])
            if t < Y_ON_SCALAR:
                nc.scalar.activation(win_ya[t][:, :S], y_bank[:], ACT.Copy, scale=gn_t[:, t : t + 1])
            else:
                nc.vector.tensor_scalar(win_ya[t][:, :S], y_bank[:], gn_t[:, t : t + 1], None, ALU.mult)
            nc.gpsimd.tensor_scalar(ycopy[t], win_ya[t][:, :S], 1.0, 0.0, ALU.mult, ALU.add)
        d_bank = []
        for t in range(PLANES):
            d_bank.append(psum.tile([P, S], F32, name=f"d_bank{t}", tag=f"db{t}"))
            product_plane(d_bank[t][:], w2[:].bitcast(FP4X4), w2s, t, xw_two[:], xs_two[:])
            nc.scalar.activation(absd[t], d_bank[t][:], ACT.Abs)
        for t in range(PLANES):
            nc.scalar.activation(win_db[t][:, :S], absd[t], ACT.Ln, bias=0.5)

        w3 = deal_w_words("w3", w3raw)
        w3s = deal(nc.gpsimd, "w3s", wsraw[2], U8)
        xs_cand = gather_scales("xs_cand", l_cand)
        xw_cand = gather_words("xw_cand", l_cand)
        cw = deal(nc.vector, "cw", xw_cand, U32)
        cs = deal(nc.vector, "cs", xs_cand, U8)

        stage = sb("stage", [P, PLANES, S], F32)
        for t in range(PLANES):
            nc.vector.tensor_tensor(stage[:, t, :], win_ya[t][:].indirect(l_n1[:]), ycopy[t], ALU.subtract)
        for t in range(PLANES):
            nc.scalar.activation(th[t], stage[:, t, :], ACT.Tanh, scale=gn_inv[:, t : t + 1])
        zf = sb("zf", [P, PLANES, S], F32)
        for t in range(PLANES):
            nc.vector.tensor_tensor(zf[:, t, :], win_ya[t][:].indirect(l_n2[:]), th[t], ALU.mult)
        zb = sb("zb", [P, PLANES * S], BF16)
        interleave(nc.vector.tensor_copy, zb[:], zf[:])
        for t in range(PLANES):
            nc.scalar.activation(stage[:, t, :], win_db[t][:].indirect(l_n3[:]), ACT.Exp, scale=-1.0)
        zq = sb("zq", [P, S], U32)
        zs = sb("zs", [P, S], U8)
        nc.vector.quantize_mx(out=zq[:].bitcast(FP8X4), scales=zs[:], in_=zb[:])
        a_bank = []
        acopy = [sb(f"acopy{t}", [P, S], F32) for t in range(N5_ON_VECTOR)]
        for t in range(PLANES):
            a_bank.append(psum.tile([P, S], F32, name=f"a_bank{t}", tag=f"ya{t}"))
            product_plane(a_bank[t][:], w3[:].bitcast(FP4X4), w3s, t, zq[:], zs[:])
            nc.scalar.copy(win_ya[t][:, :S], a_bank[t][:])
            if t < N5_ON_VECTOR:
                nc.sync.dma_start(acopy[t][:], win_ya[t][:, :S])

        z2p = zb[:].rearrange("p (t n) -> p t n", t=PLANES)
        for t in range(PLANES):
            nc.vector.scalar_tensor_tensor(z2p[:, t, :], d_bank[t][:], gs_t[:, t : t + 1], stage[:, t, :], ALU.mult, ALU.mult)
        z2b = sb("z2b", [P, PLANES * S], BF16)
        interleave(nc.vector.tensor_copy, z2b[:], z2p)
        z2q = sb("z2q", [P, S], U32)
        z2s = sb("z2s", [P, S], U8)
        nc.vector.quantize_mx(out=z2q[:].bitcast(FP8X4), scales=z2s[:], in_=z2b[:])
        b16_bank = []
        for t in range(PLANES):
            b16_bank.append(psum.tile([P, S], F32, name=f"b16_bank{t}", tag=f"db{t}"))
            product_plane(b16_bank[t][:], cw[:].bitcast(FP8X4), cs, t, z2q[:], z2s[:])

        a4 = sb("a4", [P, PLANES, S], F32)
        a5 = sb("a5", [P, PLANES - N5_ON_VECTOR, S], F32)
        d4 = sb("d4", [P, PLANES, S], F32)
        d5 = sb("d5", [P, PLANES, S], F32)
        first = sb("first", [P, PLANES, S], F32)
        b6 = [sb(f"b6_{h}", [P, PLANES, HALF], F32) for h in range(HALVES)]
        for t in range(PLANES):
            nc.scalar.activation(a4[:, t, :], win_ya[t][:].indirect(l_n4[:]), ACT.Copy)
        for t in range(N5_ON_VECTOR, PLANES):
            nc.scalar.activation(a5[:, t - N5_ON_VECTOR, :], win_ya[t][:].indirect(l_n5[:]), ACT.Copy)
        for t in range(N5_ON_VECTOR):
            nc.vector.tensor_tensor(d5[:, t, :], win_ya[t][:].indirect(l_n5[:]), acopy[t][:], ALU.subtract)
        for t in range(PLANES):
            nc.vector.tensor_tensor(d4[:, t, :], a4[:, t, :], a_bank[t][:], ALU.subtract)
        for t in range(N5_ON_VECTOR, PLANES):
            nc.vector.tensor_tensor(d5[:, t, :], a5[:, t - N5_ON_VECTOR, :], a_bank[t][:], ALU.subtract)
        for t in range(PLANES):
            nc.scalar.activation(win_db[t][:, :S], b16_bank[t][:], ACT.Copy, scale=0.5 / 16)
        for t in range(PLANES):
            nc.vector.scalar_tensor_tensor(first[:, t, :], b16_bank[t][:], 1.0 / 16, d4[:, t, :], ALU.mult, ALU.mult)
        for h in range(HALVES):
            n6_half = l_n6[:, h * HALF // GROUP : (h + 1) * HALF // GROUP]
            for t in range(PLANES):
                nc.scalar.activation(b6[h][:, t, :], win_db[t][:].indirect(n6_half), ACT.Copy)

        oq = sb("oq", [P, S], U32)
        osc = sb("osc", [P, S], U8)
        out_rows = out_0.rearrange("(p t) n -> p t n", t=PLANES)
        out_words = out_1[0].rearrange("p n r -> p (n r)").bitcast(I32)
        second = sb("second", [P, PLANES, HALF], F32)
        ob = []
        for h in range(HALVES):
            res = sb(f"res{h}", [P, PLANES, HALF], F32)
            ob.append(sb(f"ob{h}", [P, PLANES * HALF], BF16))
            nc.vector.tensor_tensor(second[:], b6[h][:], d5[:, :, cols(h)], ALU.mult)
            nc.vector.tensor_tensor(res[:], first[:, :, cols(h)], second[:], ALU.add)
            nc.sync.dma_start(out_rows[:, :, cols(h)], res[:])
            interleave(nc.vector.tensor_copy if h == HALVES - 1 else nc.scalar.copy, ob[h][:], res[:])
        for h in range(HALVES):
            nc.vector.quantize_mx(out=oq[:, cols(h)].bitcast(FP8X4), scales=osc[:, cols(h)], in_=ob[h][:])
            nc.sync.dma_start(out_words[:, cols(h)], oq[:, cols(h)].bitcast(I32))
        for q in range(QUADRANTS):
            queue = nc.scalar if q % 2 else nc.sync
            queue.dma_start(out_2[0, 4 * q : 4 * q + 4, :].bitcast(I32), osc[32 * q : 32 * q + 4, :].bitcast(I32))
